import numpy as np
import ml_dtypes


def mxq(x, axis, fmt="e4m3"):
    dtype, down = {"e4m3": (ml_dtypes.float8_e4m3fn, 7), "e5m2": (ml_dtypes.float8_e5m2, 14)}[fmt]
    v = np.moveaxis(np.asarray(x, np.float32).astype(ml_dtypes.bfloat16).astype(np.float64), axis, -1)
    blocks = v.reshape(v.shape[:-1] + (-1, 32))
    amax = np.abs(blocks).max(-1, keepdims=True)
    byte = np.maximum(np.where(amax > 0, np.frexp(amax)[1] - 1 + 127, 0) - down, 1)
    scale = np.exp2(byte - 127.0)
    codes = (blocks / scale).astype(np.float32).astype(dtype).astype(np.float64)
    return np.moveaxis((codes * scale).reshape(v.shape), -1, axis)


WIDE = False


def mx_kscale(k):
    if not WIDE:
        return np.ones(k)
    levels = np.array([10, -10, 5, -5, 0])
    if k % 512:
        return np.exp2(np.random.permutation(np.resize(levels, k // 32))).repeat(32)
    a = np.empty((k // 512, 16))
    for p in range(k // 512):
        a[p, :8] = np.random.permutation(np.resize(levels, 8))
        for g in range(8):
            far = levels[np.abs(levels - a[p, g]) >= 10]
            a[p, g + 8] = far[np.random.randint(len(far))]
    return np.exp2(a.ravel()).repeat(32)


BF16 = ml_dtypes.bfloat16


def bf(x):
    return np.asarray(x, np.float32).astype(BF16)


def f64(x):
    return np.asarray(x).astype(np.float64)


E2M1 = np.array([0.0, 0.5, 1.0, 1.5, 2.0, 3.0, 4.0, 6.0, -0.0, -0.5, -1.0, -1.5, -2.0, -3.0, -4.0, -6.0])


def pack_weight(w, fmt):
    k, n = w.shape
    w = f64(bf(w)).reshape(k // 32, 32, n)
    amax = np.abs(w).max(1)
    if fmt == "e4m3":
        byte = np.frexp(amax)[1] - 1 + 127 - 7
    else:
        mant, ex = np.frexp(amax / 6.0)
        byte = np.where(mant > 0.5, ex, ex - 1) + 127
    byte = np.clip(np.where(amax > 0, byte, 1), 1, 254)
    scaled = (w * np.exp2(127.0 - byte)[:, None, :]).reshape(k, n).astype(np.float32)
    by_word = np.ascontiguousarray(scaled.reshape(k // 512, 128, 4, n).transpose(0, 1, 3, 2))
    if fmt == "e4m3":
        words = by_word.astype(ml_dtypes.float8_e4m3fn).view(np.uint8)
    else:
        c = by_word.astype(ml_dtypes.float4_e2m1fn).view(np.uint8) & 0xF
        words = c[..., 0::2] | (c[..., 1::2] << 4)
    return np.ascontiguousarray(words), np.ascontiguousarray(byte.astype(np.uint8).reshape(k // 512, 16, n))


def unpack_weight(words, scales, fmt):
    g, p, n, _ = words.shape
    if fmt == "e4m3":
        vals = np.ascontiguousarray(words).view(ml_dtypes.float8_e4m3fn).astype(np.float64)
    else:
        nib = np.empty((g, p, n, 4), np.uint8)
        nib[..., 0::2] = words & 0xF
        nib[..., 1::2] = words >> 4
        vals = E2M1[nib]
    vals = vals * np.repeat(np.exp2(scales.astype(np.float64) - 127.0), 8, axis=1)[..., None]
    return vals.transpose(0, 1, 3, 2).reshape(g * 512, n)
def pack4(w):
    words, scales = pack_weight(w, "e2m1")
    return words.reshape(words.shape[0], 128, -1), scales


def unpack4(words, scales):
    return unpack_weight(words.reshape(words.shape[0], 128, -1, 2), scales, "e2m1")


def planes(Y):
    n, m = Y.shape
    b = f64(bf(Y)).reshape(n // 32, 32, m)
    amax = np.abs(b).max(1)
    byte = np.clip(np.where(amax > 0, np.frexp(amax)[1] - 1 + 127 - 7, 1), 1, 254)
    codes = (b * np.exp2(127.0 - byte)[:, None, :]).reshape(n, m).astype(np.float32).astype(ml_dtypes.float8_e4m3fn).view(np.uint8)
    words = codes.reshape(n // 512, 128, 4, m).transpose(0, 1, 3, 2)
    return np.ascontiguousarray(words), np.ascontiguousarray(byte.astype(np.uint8).reshape(n // 512, 16, m))


M, F, C = 1536, 512, 1024

def setup_inputs():
    n = np.random.randn
    a, b = mx_kscale(F), mx_kscale(C)
    raw = np.exp(0.5 * n(F, C))
    spectra = 0.7 * (raw - raw.mean(axis=1, keepdims=True)) / np.sqrt(F)
    bright = np.exp(0.9 * n(C))
    var0 = bright * np.exp(0.3 * n(M, C)) + 0.2
    var1 = bright * np.exp(0.3 * n(M, C)) + 0.2
    scene = 0.8 * n(M, C)
    P0 = scene + 0.5 * np.sqrt(var0) * n(M, C)
    P1 = scene + 0.5 * np.sqrt(var1) * n(M, C)
    u_words, u_scales = pack4(spectra.T / b[:, None])
    return {"A0": bf(n(M, F) * a), "S": bf(spectra / a[:, None]),
            "u_words": u_words, "u_scales": u_scales,
            "step": bf(0.42 * (1 + 0.1 * n(F)) * a),
            "P0": bf(P0), "V0": bf(b / var0), "P1": bf(P1), "V1": bf(1 / var1)}

def reference(A0, S, u_words, u_scales, step, P0, V0, P1, V1):
    A0, S, step = f64(A0), f64(S), f64(step)
    P0, V0, P1, V1 = f64(P0), f64(V0), f64(P1), f64(V1)
    U = unpack4(u_words, u_scales)
    Sq = mxq(S, 0, "e4m3")
    E = V0 * (P0 - (mxq(A0, 1, "e4m3") @ Sq))
    A1 = A0 + step * (mxq(E, 1, "e4m3") @ U)
    y = V1 * (P1 - (mxq(A1, 1, "e4m3") @ Sq))
    words, scales = planes(y.T)
    return y, words, scales

@@ -1,0 +1,485 @@
+from contextlib import ExitStack
+
+import concourse.mybir as mybir
+from concourse.masks import make_identity
+
+M, F, C = 1536, 512, 1024
+FLOPS = 3 * 2 * M * F * C
+
+F32 = mybir.dt.float32
+BF16 = mybir.dt.bfloat16
+I32 = mybir.dt.int32
+U32 = mybir.dt.uint32
+U8 = mybir.dt.uint8
+FP8X4 = mybir.dt.float8_e4m3fn_x4
+FP4X4 = mybir.dt.float4_e2m1fn_x4
+MULT = mybir.AluOpType.mult
+ADD = mybir.AluOpType.add
+SUB = mybir.AluOpType.subtract
+
+P = 128
+NT = M // P
+G = C // 512
+PAIR = 2
+IN0_RING = 4
+FIRST_V = 8
+GSPLIT = 576
+GSPLIT2 = 704
+FILL = (0, 0, 320, 320, 512)
+WORD_STORES = (4, 8, 11, 12)
+SCALE_STORES = (8, 12)
+
+
+def tile_poisson_weighted_unmixing_residual_k1_kernel(
+    tc, A0, S, u_words, u_scales, step, P0, V0, P1, V1, out_0, out_1, out_2
+):
+    nc = tc.nc
+    with ExitStack() as ctx:
+        sb = ctx.enter_context(tc.tile_pool(name="sb", bufs=1))
+        ps = ctx.enter_context(tc.psum_pool(name="ps", bufs=1))
+
+        def ring(name, n, shape, dtype):
+            return [sb.tile(shape, dtype, name="%s%d" % (name, i), align_bytes=64) for i in range(n)]
+
+        def one(name, shape, dtype):
+            return ring(name, 1, shape, dtype)[0]
+
+        ident = one("ident", [P, P], F32)
+        step_sb = one("step", [P, 4], BF16)
+        uw_raw = one("uw_raw", [P, G, 2 * F], U8)
+        us_raw = one("us_raw", [P, G, F], U8)
+        uw = one("uw", [P, G, 4, 2 * P], U8)
+        us = one("us", [P, G, 4, P], U8)
+        s_raw = ring("s_raw", G, [P, 4, 512], BF16)
+        s_grp = ring("s_grp", G, [P, 512, 4], BF16)
+        s_q = ring("s_q", G, [P, 512], U32)
+        s_sc = ring("s_sc", G, [P, 512], U8)
+        a0 = one("a0", [P, NT, F], BF16)
+        p0 = ring("p0_", IN0_RING, [P, PAIR, C], BF16)
+        v0 = ring("v0_", IN0_RING, [P, PAIR, C], BF16)
+        p1 = ring("p1_", NT // PAIR - 1, [P, PAIR, C], BF16)
+        v1 = ring("v1_", NT // PAIR, [P, PAIR, C], BF16)
+        wide = ring("wide", NT, [P, C], F32)
+        d1 = ring("d1_", 4, [P, C], F32)
+        a0t = ring("a0t", 4, [P, PAIR, P, 4], BF16)
+        a0q = ring("a0q", 2, [P, PAIR, P], U32)
+        a0s = ring("a0s", 2, [P, PAIR, P], U8)
+        e_bf = ring("e_bf", 2, [P, C], BF16)
+        e_t = ring("e_t", 2, [P, G, P, 4], BF16)
+        e_q = ring("e_q", 2, [P, G, P], U32)
+        e_s = ring("e_s", 2, [P, G, P], U8)
+        a1 = ring("a1_", 2, [P, 4, P], BF16)
+        a1t = ring("a1t", 2, [P, P, 4], BF16)
+        a1q = ring("a1q", 2, [P, P], U32)
+        a1s = ring("a1s", 2, [P, P], U8)
+        y_bf = ring("y_bf", 3, [P, C], BF16)
+        y_t = ring("y_t", 3, [P, G, P, 4], BF16)
+        y_q = one("y_q", [P, G, M], U32)
+        y_s = one("y_s", [P, G, M], U8)
+
+        r0 = [ps.tile([P, 512], F32, name="r0_%d" % h) for h in range(G)]
+        r1 = [ps.tile([P, 512], F32, name="r1_%d" % h) for h in range(G)]
+        grad = ps.tile([P, 4, P], F32, name="grad")
+        ps_a = ps.tile([P, PAIR, 2, P], F32, name="ps_a")
+        ps_e = ps.tile([P, G, 2, P], F32, name="ps_e")
+        ps_y = ps.tile([P, G, 2, P], F32, name="ps_y")
+
+        def pick(tiles, k):
+            return tiles[k % len(tiles)]
+
+        def rows(tiles, k):
+            return pick(tiles, k // PAIR)[:, k % PAIR, :]
+
+        def half(h):
+            return slice(512 * h, 512 * (h + 1))
+
+        def y_of(k):
+            return pick(d1, k - 1) if k in (9, 10) else pick(wide, k + 4)
+
+        def res1(k):
+            return r0 if k in (9, 11) else r1
+
+        def words(t):
+            return t[:].rearrange("p g m t -> p (g m t)").bitcast(F32).rearrange("p (g m u) -> p g m u", g=G, u=2)
+
+        def load_rows(tiles, src, k0, n):
+            dst = pick(tiles, k0 // PAIR)[:, k0 % PAIR : k0 % PAIR + n, :]
+            nc.sync.dma_start(out=dst, in_=src[P * k0 : P * (k0 + n), :].rearrange("(k p) c -> p k c", p=P))
+
+        def load_a0(k0, k1):
+            nc.sync.dma_start(out=a0[:, k0:k1, :], in_=A0[P * k0 : P * k1, :].rearrange("(k p) f -> p k f", p=P))
+
+        def interleave_s(engine_copy, q):
+            h, cols = q // 2, slice(256 * (q % 2), 256 * (q % 2 + 1))
+            engine_copy(out=s_grp[h][:, cols, :].rearrange("p (c i) j -> p c j i", i=4),
+                        in_=s_raw[h][:, :, cols].rearrange("p j (c i) -> p c j i", i=4))
+
+        def quant_s(h):
+            nc.vector.quantize_mx(out=s_q[h][:].bitcast(FP8X4), scales=s_sc[h][:], in_=s_grp[h][:].rearrange("p c j -> p (c j)"))
+
+        def turn_a0(c):
+            for j in range(PAIR):
+                w = a0[:, PAIR * c + j, :].bitcast(F32)
+                for u in range(2):
+                    nc.tensor.transpose(ps_a[:, j, u, :], w[:, u::2], ident[:])
+
+        def copy_a0(c):
+            nc.scalar.copy(out=words(pick(a0t, c)), in_=ps_a[:].rearrange("p j u m -> p j m u"))
+
+        def quant_a0(c):
+            nc.vector.quantize_mx(out=pick(a0q, c)[:].rearrange("p j m -> p (j m)").bitcast(FP8X4),
+                                  scales=pick(a0s, c)[:].rearrange("p j m -> p (j m)"),
+                                  in_=pick(a0t, c)[:].rearrange("p j m t -> p (j m t)"))
+
+        def spectra_mm(banks, codes, scales, h):
+            nc.tensor.matmul_mx(out=banks[h][:], lhsT=codes.bitcast(FP8X4), lhsT_scale=scales,
+                                rhs=s_q[h][:].bitcast(FP8X4), rhs_scale=s_sc[h][:], start=True, stop=True)
+
+        def mm1(k):
+            for h in range(G):
+                spectra_mm(r0, rows(a0q, k), rows(a0s, k), h)
+
+        def sub0(k, h):
+            nc.vector.tensor_tensor(out=wide[k][:, half(h)], in0=rows(p0, k)[:, half(h)], in1=r0[h][:], op=SUB)
+
+        def weigh0(engine, k, cols):
+            engine.tensor_tensor(out=pick(e_bf, k)[:, cols], in0=wide[k][:, cols], in1=rows(v0, k)[:, cols], op=MULT)
+
+        def turn_e(k):
+            w = pick(e_bf, k)[:].bitcast(F32)
+            for g in range(G):
+                for u in range(2):
+                    nc.tensor.transpose(ps_e[:, g, u, :], w[:, 256 * g + u : 256 * (g + 1) : 2], ident[:])
+
+        def copy_e(k):
+            nc.scalar.copy(out=words(pick(e_t, k)), in_=ps_e[:].rearrange("p g u m -> p g m u"))
+
+        def quant_e(k):
+            nc.vector.quantize_mx(out=pick(e_q, k)[:].rearrange("p g m -> p (g m)").bitcast(FP8X4),
+                                  scales=pick(e_s, k)[:].rearrange("p g m -> p (g m)"),
+                                  in_=pick(e_t, k)[:].rearrange("p g m t -> p (g m t)"))
+
+        def mm2(k):
+            for t in range(4):
+                for g in range(G):
+                    nc.tensor.matmul_mx(out=grad[:, t, :], lhsT=uw[:, g, t, :].bitcast(FP4X4), lhsT_scale=us[:, g, t, :],
+                                        rhs=pick(e_q, k)[:, g, :].bitcast(FP8X4), rhs_scale=pick(e_s, k)[:, g, :],
+                                        start=(g == 0), stop=(g == G - 1))
+
+        def update(k):
+            for t in range(4):
+                nc.vector.scalar_tensor_tensor(out=pick(a1, k)[:, t, :], in0=grad[:, t, :], scalar=step_sb[:, t : t + 1],
+                                               in1=pick(a0t, k // PAIR)[:, k % PAIR, :, t], op0=MULT, op1=ADD)
+
+        def interleave_a1(k):
+            nc.scalar.copy(out=pick(a1t, k)[:].rearrange("p (m i) t -> p m t i", i=4),
+                           in_=pick(a1, k)[:].rearrange("p t (m i) -> p m t i", i=4))
+
+        def quant_a1(k):
+            nc.vector.quantize_mx(out=pick(a1q, k)[:].bitcast(FP8X4), scales=pick(a1s, k)[:], in_=pick(a1t, k)[:].rearrange("p m t -> p (m t)"))
+
+        def mm3(k):
+            for h in range(G):
+                spectra_mm(res1(k), pick(a1q, k)[:], pick(a1s, k)[:], h)
+
+        def sub1(k, h):
+            nc.vector.tensor_tensor(out=pick(d1, k)[:, half(h)], in0=rows(p1, k)[:, half(h)], in1=res1(k)[h][:], op=SUB)
+
+        def weigh1(engine, k, cols):
+            engine.tensor_tensor(out=y_of(k)[:, cols], in0=pick(d1, k)[:, cols], in1=rows(v1, k)[:, cols], op=MULT)
+
+        def pair_order(ap):
+            return ap.rearrange("m (q u e) -> m u q e", u=2, e=2)
+
+        def weigh1_rounded(k, g):
+            dst = pick(y_bf, k)[:].rearrange("m (u q e) -> m u q e", u=2, e=2)[:, :, P * g : P * (g + 1), :]
+            nc.vector.tensor_tensor(out=dst, in0=pair_order(pick(d1, k)[:, half(g)]), in1=pair_order(rows(v1, k)[:, half(g)]), op=MULT)
+
+        def store_y(k):
+            nc.sync.dma_start(out=out_0[P * k : P * (k + 1), :], in_=y_of(k)[:])
+
+        def round_y(k):
+            nc.scalar.copy(out=pick(y_bf, k)[:].rearrange("m (u q e) -> m u q e", u=2, e=2),
+                           in_=pair_order(y_of(k)[:]))
+
+        def y_bank(k, g):
+            if k < 8:
+                return ps_y
+            return (ps_y, ps_a, ps_e)[(k + (g if k == NT - 1 else 0)) % 3]
+
+        def turn_y(k, gs=range(G)):
+            w = pick(y_bf, k)[:].bitcast(F32)
+            for g in gs:
+                for u in range(2):
+                    nc.tensor.transpose(y_bank(k, g)[:, g, u, :], w[:, 256 * u + P * g : 256 * u + P * (g + 1)], ident[:])
+
+        def copy_y(k, gs=range(G)):
+            sel = slice(gs[0], gs[-1] + 1)
+            nc.scalar.copy(out=words(pick(y_t, k))[:, sel], in_=y_bank(k, gs[0])[:, sel].rearrange("p g u m -> p g m u"))
+
+        def quant_y(k, gs=range(G)):
+            cols = slice(P * k, P * (k + 1))
+            for g in gs:
+                nc.vector.quantize_mx(out=y_q[:, g, cols].bitcast(FP8X4), scales=y_s[:, g, cols],
+                                      in_=pick(y_t, k)[:, g, :, :].rearrange("p m t -> p (m t)"))
+
+        def store_planes(k):
+            if k + 1 in WORD_STORES:
+                i = WORD_STORES.index(k + 1)
+                cols = slice(P * (WORD_STORES[i - 1] if i else 0), P * (k + 1))
+                dst = out_1.rearrange("g p m t -> p g (m t)").bitcast(I32)
+                nc.sync.dma_start(out=dst[:, :, cols], in_=y_q[:, :, cols].bitcast(I32))
+            if k + 1 in SCALE_STORES:
+                i = SCALE_STORES.index(k + 1)
+                cols = slice(P * (SCALE_STORES[i - 1] if i else 0), P * (k + 1))
+                for q in range(4):
+                    dst = out_2[:, 4 * q : 4 * q + 4, cols].rearrange("g r m -> r g m")
+                    nc.sync.dma_start(out=dst.bitcast(I32), in_=y_s[32 * q : 32 * q + 4, :, cols].bitcast(I32))
+
+        def sort_u_words():
+            nc.vector.tensor_copy(out=uw[:].rearrange("p g t (m b) -> p g t m b", b=2),
+                                  in_=uw_raw[:].rearrange("p g (m t b) -> p g t m b", t=4, b=2))
+
+        def sort_u_scales():
+            nc.vector.tensor_copy(out=us[:], in_=us_raw[:].rearrange("p g (m t) -> p g t m", t=4))
+
+        def load_u_words():
+            nc.sync.dma_start(out=uw_raw[:].bitcast(I32), in_=u_words.rearrange("g p n -> p g n").bitcast(I32))
+
+        def load_u_scales():
+            for q in range(4):
+                nc.sync.dma_start(out=us_raw[32 * q : 32 * q + 4, :, :].bitcast(I32),
+                                  in_=u_scales[:, 4 * q : 4 * q + 4, :].rearrange("g r n -> r g n").bitcast(I32))
+
+        def load_s(h):
+            nc.sync.dma_start(out=s_raw[h][:], in_=S.rearrange("(p j) c -> p j c", j=4)[:, :, half(h)])
+
+        def load_step():
+            nc.sync.dma_start(out=step_sb[:], in_=step.rearrange("(p t) -> p t", t=4))
+
+        def mm1h(k, h):
+            spectra_mm(r0, rows(a0q, k), rows(a0s, k), h)
+
+        def each(k, *stages):
+            if 0 <= k < NT:
+                for stage in stages:
+                    stage(k)
+
+        ctx.enter_context(tc.manual_schedule())
+
+        nc.vector.memset(us_raw[:].rearrange("p g n -> p (g n)").bitcast(I32), 0)
+        make_identity(nc, ident[:])
+        load_u_words()
+        load_a0(0, 2)
+        load_s(0)
+        load_s(1)
+        load_rows(p0, P0, 0, 1)
+        load_a0(2, 4)
+        load_rows(v0, V0, 0, 1)
+        load_u_scales()
+        load_rows(p0, P0, 1, 1)
+        load_rows(v0, V0, 1, 1)
+        load_step()
+        load_a0(4, 8)
+        load_rows(p0, P0, 2, 2)
+        load_rows(v0, V0, 2, 2)
+        load_rows(p0, P0, 4, 2)
+        load_rows(v0, V0, 4, 2)
+        load_rows(p1, P1, 0, 2)
+        load_rows(v1, V1, 0, 2)
+        load_rows(p0, P0, 6, 2)
+        load_rows(v0, V0, 6, 2)
+        load_a0(8, 12)
+        load_rows(p1, P1, 2, 2)
+        load_rows(v1, V1, 2, 2)
+
+        turn_a0(0)
+        copy_a0(0)
+        sort_u_words()
+        interleave_s(nc.vector.tensor_copy, 0)
+        interleave_s(nc.vector.tensor_copy, 1)
+        quant_a0(0)
+        interleave_s(nc.scalar.copy, 3)
+        interleave_s(nc.vector.tensor_copy, 2)
+        turn_a0(1)
+        quant_s(0)
+        quant_s(1)
+        mm1h(0, 0)
+        sort_u_scales()
+        sub0(0, 0)
+        mm1h(0, 1)
+        sub0(0, 1)
+        mm1(1)
+        copy_a0(1)
+        turn_a0(2)
+        weigh0(nc.vector, 0, slice(0, 1024))
+        sub0(1, 1)
+        turn_e(0)
+        sub0(1, 0)
+        copy_e(0)
+        quant_a0(1)
+        weigh0(nc.vector, 1, slice(0, 1024))
+        load_rows(p0, P0, 8, 2)
+        load_rows(v0, V0, 8, 2)
+        load_rows(p1, P1, 4, 2)
+        load_rows(v1, V1, 4, 2)
+        copy_a0(2)
+        mm1(2)
+        quant_e(0)
+        sub0(2, 0)
+        mm2(0)
+        sub0(2, 1)
+        turn_e(1)
+        copy_e(1)
+        update(0)
+        weigh0(nc.vector, 2, slice(320, 1024))
+        mm1(3)
+        weigh0(nc.gpsimd, 2, slice(0, 320))
+        interleave_a1(0)
+        turn_a0(3)
+        quant_e(1)
+        quant_a0(2)
+        copy_a0(3)
+        sub0(3, 0)
+        mm2(1)
+        turn_e(2)
+        quant_a1(0)
+        sub0(3, 1)
+        copy_e(2)
+        mm3(0)
+        update(1)
+        weigh0(nc.vector, 3, slice(320, 1024))
+        quant_e(2)
+        mm1(4)
+        sub0(4, 1)
+        weigh0(nc.gpsimd, 3, slice(0, 320))
+        load_rows(p0, P0, 10, 2)
+        load_rows(v0, V0, 10, 2)
+        load_rows(p1, P1, 6, 2)
+        load_rows(v1, V1, 6, 2)
+        sub0(4, 0)
+        interleave_a1(1)
+        turn_e(3)
+        weigh0(nc.gpsimd, 4, slice(0, 512))
+        mm2(2)
+        quant_a1(1)
+        sub1(0, 1)
+        mm1(5)
+        sub1(0, 0)
+        copy_e(3)
+        update(2)
+        quant_a0(3)
+        mm3(1)
+        quant_e(3)
+        interleave_a1(2)
+        mm2(3)
+        weigh0(nc.vector, 4, slice(512, 1024))
+        for s in range(5, NT - 1):
+            if s in (6, 8):
+                load_rows(p1, P1, s + 2, PAIR)
+                load_rows(v1, V1, s + 2, PAIR)
+            weigh1(nc.gpsimd, s - 5, slice(0, C))
+            each(s - 1, turn_e, copy_e)
+            for h in range(G):
+                sub0(s, h)
+            mm1(s + 1)
+            each(s - 6, turn_y, copy_y)
+            if s in (5, 7):
+                turn_a0((s + 3) // 2)
+                copy_a0((s + 3) // 2)
+            for h in range(G):
+                sub1(s - 4, h)
+            update(s - 2)
+            each(s - 5, store_y, round_y)
+            interleave_a1(s - 2)
+            each(s - 3, quant_a1, mm3)
+            each(s - 1, quant_e, mm2)
+            if s in (6, 8):
+                quant_a0(s // 2 + 1)
+            each(s - 6, quant_y, store_planes)
+            if s < NT - 2:
+                weigh0(nc.vector, s, slice(0, C))
+        weigh0(nc.vector, 10, slice(0, 1024))
+        sub1(7, 0)
+        sub1(7, 1)
+        update(9)
+        sub0(11, 0)
+        weigh1(nc.gpsimd, 6, slice(0, 1024))
+        turn_y(5)
+        copy_y(5)
+        sub0(11, 1)
+        quant_a1(8)
+        interleave_a1(9)
+        turn_e(10)
+        mm3(8)
+        copy_e(10)
+        quant_a1(9)
+        quant_y(5)
+        quant_e(10)
+        mm2(10)
+        weigh0(nc.vector, 11, slice(0, 1024))
+        sub1(8, 0)
+        turn_e(11)
+        mm3(9)
+        round_y(6)
+        sub1(8, 1)
+        copy_e(11)
+        update(10)
+        interleave_a1(10)
+        weigh1(nc.gpsimd, 7, slice(0, 1024))
+        turn_y(6)
+        sub1(9, 0)
+        sub1(9, 1)
+        quant_e(11)
+        mm2(11)
+        quant_a1(10)
+        copy_y(6)
+        mm3(10)
+        round_y(7)
+        weigh1(nc.vector, 8, slice(0, 1024))
+        store_y(6)
+        quant_y(6)
+        turn_y(7)
+        update(11)
+        sub1(10, 0)
+        round_y(8)
+        interleave_a1(11)
+        weigh1(nc.vector, 9, slice(576, 1024))
+        copy_y(7)
+        quant_a1(11)
+        sub1(10, 1)
+        quant_y(7)
+        mm3(11)
+        store_y(8)
+        store_y(7)
+        turn_y(8)
+        weigh1(nc.gpsimd, 9, slice(0, 576))
+        weigh1(nc.gpsimd, 10, slice(704, 1024))
+        round_y(9)
+        sub1(11, 0)
+        weigh1(nc.vector, 10, slice(0, 704))
+        round_y(10)
+        turn_y(9)
+        sub1(11, 1)
+        weigh1_rounded(11, 0)
+        weigh1(nc.vector, 11, slice(0, 1024))
+        copy_y(8)
+        turn_y(10)
+        weigh1_rounded(11, 1)
+        copy_y(9)
+        turn_y(11, [0])
+        copy_y(10)
+        quant_y(8)
+        store_planes(7)
+        store_y(10)
+        copy_y(11, [0])
+        turn_y(11, [1])
+        quant_y(9)
+        quant_y(10)
+        copy_y(11, [1])
+        store_y(9)
+        store_y(11)
+        quant_y(11, [1])
+        store_planes(10)
+        quant_y(11, [0])
+        store_planes(11)

@@ -23,6 +23,7 @@ G = C // 512
 PAIR = 2
 IN0_RING = 4
 FIRST_V = 8
+HALVES = (0, 1)
 GSPLIT = 576
 GSPLIT2 = 704
 FILL = (0, 0, 320, 320, 512)
@@ -91,7 +92,7 @@ def tile_poisson_weighted_unmixing_residual_k1_kernel(
             return pick(tiles, k // PAIR)[:, k % PAIR, :]
 
         def half(h):
-            return slice(512 * h, 512 * (h + 1))
+            return slice(0, C) if h is None else slice(512 * h, 512 * (h + 1))
 
         def y_of(k):
             return pick(d1, k - 1) if k in (9, 10) else pick(wide, k + 4)
@@ -273,7 +274,10 @@ def tile_poisson_weighted_unmixing_residual_k1_kernel(
         load_a0(0, 2)
         load_s(0)
         load_s(1)
+        sort_u_words()
         load_rows(p0, P0, 0, 1)
+        interleave_s(nc.vector.tensor_copy, 1)
+        interleave_s(nc.vector.tensor_copy, 0)
         load_a0(2, 4)
         load_rows(v0, V0, 0, 1)
         load_u_scales()
@@ -286,92 +290,88 @@ def tile_poisson_weighted_unmixing_residual_k1_kernel(
         load_rows(p0, P0, 4, 2)
         load_rows(v0, V0, 4, 2)
         load_rows(p1, P1, 0, 2)
+        turn_a0(0)
         load_rows(v1, V1, 0, 2)
         load_rows(p0, P0, 6, 2)
+        interleave_s(nc.vector.tensor_copy, 2)
+        quant_s(0)
         load_rows(v0, V0, 6, 2)
-        load_a0(8, 12)
-        load_rows(p1, P1, 2, 2)
-        load_rows(v1, V1, 2, 2)
-
-        turn_a0(0)
         copy_a0(0)
-        sort_u_words()
-        interleave_s(nc.vector.tensor_copy, 0)
-        interleave_s(nc.vector.tensor_copy, 1)
+        load_a0(8, 12)
         quant_a0(0)
         interleave_s(nc.scalar.copy, 3)
-        interleave_s(nc.vector.tensor_copy, 2)
-        turn_a0(1)
-        quant_s(0)
-        quant_s(1)
+        load_rows(p1, P1, 2, 2)
         mm1h(0, 0)
-        sort_u_scales()
-        sub0(0, 0)
+        quant_s(1)
         mm1h(0, 1)
+        sort_u_scales()
+        load_rows(v1, V1, 2, 2)
+        sub0(0, 0)
         sub0(0, 1)
+        weigh0(nc.vector, 0, slice(0, 1024))
+        turn_a0(1)
         mm1(1)
         copy_a0(1)
-        turn_a0(2)
-        weigh0(nc.vector, 0, slice(0, 1024))
-        sub0(1, 1)
         turn_e(0)
-        sub0(1, 0)
         copy_e(0)
+        sub0(1, 1)
+        sub0(1, 0)
         quant_a0(1)
         weigh0(nc.vector, 1, slice(0, 1024))
         load_rows(p0, P0, 8, 2)
-        load_rows(v0, V0, 8, 2)
-        load_rows(p1, P1, 4, 2)
-        load_rows(v1, V1, 4, 2)
-        copy_a0(2)
-        mm1(2)
         quant_e(0)
+        turn_a0(2)
+        copy_a0(2)
+        load_rows(v0, V0, 8, 2)
+        mm1(2)
         sub0(2, 0)
-        mm2(0)
         sub0(2, 1)
+        mm2(0)
         turn_e(1)
-        copy_e(1)
         update(0)
         weigh0(nc.vector, 2, slice(320, 1024))
-        mm1(3)
-        weigh0(nc.gpsimd, 2, slice(0, 320))
-        interleave_a1(0)
-        turn_a0(3)
+        load_rows(p1, P1, 4, 2)
+        copy_e(1)
         quant_e(1)
+        turn_a0(3)
+        load_rows(v1, V1, 4, 2)
+        interleave_a1(0)
         quant_a0(2)
         copy_a0(3)
-        sub0(3, 0)
+        mm1(3)
         mm2(1)
-        turn_e(2)
+        sub0(3, 0)
+        weigh0(nc.gpsimd, 2, slice(0, 320))
         quant_a1(0)
+        turn_e(2)
         sub0(3, 1)
-        copy_e(2)
-        mm3(0)
         update(1)
         weigh0(nc.vector, 3, slice(320, 1024))
+        copy_e(2)
         quant_e(2)
-        mm1(4)
-        sub0(4, 1)
         weigh0(nc.gpsimd, 3, slice(0, 320))
+        mm3(0)
+        mm1(4)
+        quant_a0(3)
+        interleave_a1(1)
+        quant_a1(1)
+        sub0(4, 0)
         load_rows(p0, P0, 10, 2)
+        sub1(0, 1)
+        mm2(2)
+        sub1(0, 0)
         load_rows(v0, V0, 10, 2)
         load_rows(p1, P1, 6, 2)
         load_rows(v1, V1, 6, 2)
-        sub0(4, 0)
-        interleave_a1(1)
         turn_e(3)
+        sub0(4, 1)
         weigh0(nc.gpsimd, 4, slice(0, 512))
-        mm2(2)
-        quant_a1(1)
-        sub1(0, 1)
+        mm3(1)
         mm1(5)
-        sub1(0, 0)
         copy_e(3)
         update(2)
-        quant_a0(3)
-        mm3(1)
-        quant_e(3)
         interleave_a1(2)
+        quant_e(3)
         mm2(3)
         weigh0(nc.vector, 4, slice(512, 1024))
         for s in range(5, NT - 1):
@@ -379,15 +379,15 @@ def tile_poisson_weighted_unmixing_residual_k1_kernel(
                 load_rows(p1, P1, s + 2, PAIR)
                 load_rows(v1, V1, s + 2, PAIR)
             weigh1(nc.gpsimd, s - 5, slice(0, C))
-            each(s - 1, turn_e, copy_e)
-            for h in range(G):
-                sub0(s, h)
-            mm1(s + 1)
-            each(s - 6, turn_y, copy_y)
             if s in (5, 7):
                 turn_a0((s + 3) // 2)
                 copy_a0((s + 3) // 2)
-            for h in range(G):
+            each(s - 6, turn_y, copy_y)
+            each(s - 1, turn_e, copy_e)
+            for h in HALVES:
+                sub0(s, h)
+            mm1(s + 1)
+            for h in HALVES:
                 sub1(s - 4, h)
             update(s - 2)
             each(s - 5, store_y, round_y)
@@ -396,90 +396,92 @@ def tile_poisson_weighted_unmixing_residual_k1_kernel(
             each(s - 1, quant_e, mm2)
             if s in (6, 8):
                 quant_a0(s // 2 + 1)
-            each(s - 6, quant_y, store_planes)
-            if s < NT - 2:
-                weigh0(nc.vector, s, slice(0, C))
-        weigh0(nc.vector, 10, slice(0, 1024))
+            if s >= 6:
+                quant_y(s - 6, [0])
+            weigh0(nc.vector, s, slice(0, C))
+            if s >= 6:
+                quant_y(s - 6, [1])
+                store_planes(s - 6)
         sub1(7, 0)
+        sub0(11, 1)
+        turn_y(5)
+        turn_e(10)
         sub1(7, 1)
         update(9)
         sub0(11, 0)
-        weigh1(nc.gpsimd, 6, slice(0, 1024))
-        turn_y(5)
-        copy_y(5)
-        sub0(11, 1)
         quant_a1(8)
-        interleave_a1(9)
-        turn_e(10)
-        mm3(8)
+        copy_y(5)
         copy_e(10)
-        quant_a1(9)
+        interleave_a1(9)
         quant_y(5)
         quant_e(10)
-        mm2(10)
         weigh0(nc.vector, 11, slice(0, 1024))
-        sub1(8, 0)
+        weigh1(nc.gpsimd, 6, slice(0, 1024))
+        mm3(8)
+        round_y(6)
+        quant_a1(9)
+        mm2(10)
         turn_e(11)
         mm3(9)
-        round_y(6)
-        sub1(8, 1)
-        copy_e(11)
-        update(10)
-        interleave_a1(10)
         weigh1(nc.gpsimd, 7, slice(0, 1024))
+        sub1(8, 0)
         turn_y(6)
+        copy_e(11)
+        sub1(8, 1)
+        update(10)
         sub1(9, 0)
-        sub1(9, 1)
-        quant_e(11)
-        mm2(11)
-        quant_a1(10)
+        interleave_a1(10)
         copy_y(6)
-        mm3(10)
+        sub1(9, 1)
         round_y(7)
-        weigh1(nc.vector, 8, slice(0, 1024))
-        store_y(6)
-        quant_y(6)
+        store_y(7)
+        quant_e(11)
+        quant_a1(10)
+        mm2(11)
         turn_y(7)
-        update(11)
-        sub1(10, 0)
+        weigh1(nc.vector, 8, slice(0, 1024))
+        weigh1(nc.gpsimd, 9, slice(0, 576))
         round_y(8)
-        interleave_a1(11)
+        quant_y(6)
+        store_y(8)
+        mm3(10)
+        update(11)
         weigh1(nc.vector, 9, slice(576, 1024))
-        copy_y(7)
+        interleave_a1(11)
         quant_a1(11)
+        copy_y(7)
+        round_y(9)
         sub1(10, 1)
         quant_y(7)
         mm3(11)
-        store_y(8)
-        store_y(7)
-        turn_y(8)
-        weigh1(nc.gpsimd, 9, slice(0, 576))
-        weigh1(nc.gpsimd, 10, slice(704, 1024))
-        round_y(9)
-        sub1(11, 0)
-        weigh1(nc.vector, 10, slice(0, 704))
-        round_y(10)
         turn_y(9)
+        store_y(9)
+        sub1(10, 0)
+        sub1(11, 0)
+        turn_y(8)
+        weigh1(nc.vector, 10, slice(0, 704))
         sub1(11, 1)
         weigh1_rounded(11, 0)
         weigh1(nc.vector, 11, slice(0, 1024))
-        copy_y(8)
-        turn_y(10)
-        weigh1_rounded(11, 1)
-        copy_y(9)
-        turn_y(11, [0])
-        copy_y(10)
-        quant_y(8)
         store_planes(7)
+        copy_y(9)
+        weigh1(nc.gpsimd, 10, slice(704, 1024))
+        weigh1_rounded(11, 1)
+        store_y(6)
+        round_y(10)
+        turn_y(10)
+        copy_y(8)
+        quant_y(8)
         store_y(10)
+        copy_y(10)
+        quant_y(9)
+        store_y(11)
+        quant_y(10)
+        turn_y(11, [0])
         copy_y(11, [0])
         turn_y(11, [1])
-        quant_y(9)
-        quant_y(10)
         copy_y(11, [1])
-        store_y(9)
-        store_y(11)
-        quant_y(11, [1])
         store_planes(10)
+        quant_y(11, [1])
         quant_y(11, [0])
         store_planes(11)

@@ -23,11 +23,18 @@ G = C // 512
 PAIR = 2
 IN0_RING = 4
 FIRST_V = 8
-HALVES = (0, 1)
+ALT0 = ()
+TURNED = range(4, 12)
+AHEAD = 3
+QY = (8, 10)
+FILL0 = 0
+FILL1 = 0
+FILL2 = 320
+FILL3 = 320
+FILL4 = 256
 GSPLIT = 576
 GSPLIT2 = 704
-FILL = (0, 0, 320, 320, 512)
-WORD_STORES = (4, 8, 11, 12)
+WORD_STORES = (4, 8, 10, 11, 12)
 SCALE_STORES = (8, 12)
 
 
@@ -51,39 +58,37 @@ def tile_poisson_weighted_unmixing_residual_k1_kernel(
         us_raw = one("us_raw", [P, G, F], U8)
         uw = one("uw", [P, G, 4, 2 * P], U8)
         us = one("us", [P, G, 4, P], U8)
-        s_raw = ring("s_raw", G, [P, 4, 512], BF16)
-        s_grp = ring("s_grp", G, [P, 512, 4], BF16)
+        stage = ring("stage", 6, [P, 2048], BF16)
+        s_raw = [stage[2 + h][:].rearrange("p (j c) -> p j c", j=4) for h in range(G)]
+        s_grp = [stage[4 + h][:].rearrange("p (c j) -> p c j", j=4) for h in range(G)]
+        codes = ring("codes", 3, [P, 512], U32)
+        scales = ring("scales", 3, [P, 512], U8)
         s_q = ring("s_q", G, [P, 512], U32)
         s_sc = ring("s_sc", G, [P, 512], U8)
         a0 = one("a0", [P, NT, F], BF16)
         p0 = ring("p0_", IN0_RING, [P, PAIR, C], BF16)
         v0 = ring("v0_", IN0_RING, [P, PAIR, C], BF16)
-        p1 = ring("p1_", NT // PAIR - 1, [P, PAIR, C], BF16)
+        p1 = ring("p1_", NT // PAIR - 2, [P, PAIR, C], BF16)
         v1 = ring("v1_", NT // PAIR, [P, PAIR, C], BF16)
         wide = ring("wide", NT, [P, C], F32)
         d1 = ring("d1_", 4, [P, C], F32)
-        a0t = ring("a0t", 4, [P, PAIR, P, 4], BF16)
-        a0q = ring("a0q", 2, [P, PAIR, P], U32)
-        a0s = ring("a0s", 2, [P, PAIR, P], U8)
+        neg_r = ring("neg_r", 2, [P, 4, P], F32)
+        v0t = ring("v0t", 3, [P, P, 4], BF16)
         e_bf = ring("e_bf", 2, [P, C], BF16)
-        e_t = ring("e_t", 2, [P, G, P, 4], BF16)
-        e_q = ring("e_q", 2, [P, G, P], U32)
-        e_s = ring("e_s", 2, [P, G, P], U8)
         a1 = ring("a1_", 2, [P, 4, P], BF16)
-        a1t = ring("a1t", 2, [P, P, 4], BF16)
-        a1q = ring("a1q", 2, [P, P], U32)
-        a1s = ring("a1s", 2, [P, P], U8)
         y_bf = ring("y_bf", 3, [P, C], BF16)
-        y_t = ring("y_t", 3, [P, G, P, 4], BF16)
+        y_t = ring("y_t", 2, [P, G, PAIR, P, 4], BF16)
         y_q = one("y_q", [P, G, M], U32)
         y_s = one("y_s", [P, G, M], U8)
 
         r0 = [ps.tile([P, 512], F32, name="r0_%d" % h) for h in range(G)]
         r1 = [ps.tile([P, 512], F32, name="r1_%d" % h) for h in range(G)]
         grad = ps.tile([P, 4, P], F32, name="grad")
-        ps_a = ps.tile([P, PAIR, 2, P], F32, name="ps_a")
+        ps_a = ps.tile([P, G, 2, P], F32, name="ps_a")
         ps_e = ps.tile([P, G, 2, P], F32, name="ps_e")
         ps_y = ps.tile([P, G, 2, P], F32, name="ps_y")
+
+        turned = ps_a[:].rearrange("p g u m -> p (g u m)")
 
         def pick(tiles, k):
             return tiles[k % len(tiles)]
@@ -97,11 +102,19 @@ def tile_poisson_weighted_unmixing_residual_k1_kernel(
         def y_of(k):
             return pick(d1, k - 1) if k in (9, 10) else pick(wide, k + 4)
 
+        def res0(k):
+            return r1 if k in ALT0 else r0
+
         def res1(k):
             return r0 if k in (9, 11) else r1
 
-        def words(t):
-            return t[:].rearrange("p g m t -> p (g m t)").bitcast(F32).rearrange("p (g m u) -> p g m u", g=G, u=2)
+        A1_COLS, A0_COLS, E_COLS = slice(0, 128), slice(128, 256), slice(256, 512)
+
+        def staged(slot, cols):
+            return pick(stage, slot)[:, 4 * cols.start : 4 * cols.stop]
+
+        def quant(slot, cols):
+            nc.vector.quantize_mx(out=pick(codes, slot)[:, cols].bitcast(FP8X4), scales=pick(scales, slot)[:, cols], in_=staged(slot, cols))
 
         def load_rows(tiles, src, k0, n):
             dst = pick(tiles, k0 // PAIR)[:, k0 % PAIR : k0 % PAIR + n, :]
@@ -116,21 +129,22 @@ def tile_poisson_weighted_unmixing_residual_k1_kernel(
                         in_=s_raw[h][:, :, cols].rearrange("p j (c i) -> p c j i", i=4))
 
         def quant_s(h):
-            nc.vector.quantize_mx(out=s_q[h][:].bitcast(FP8X4), scales=s_sc[h][:], in_=s_grp[h][:].rearrange("p c j -> p (c j)"))
+            nc.vector.quantize_mx(out=s_q[h][:].bitcast(FP8X4), scales=s_sc[h][:], in_=stage[4 + h][:])
 
-        def turn_a0(c):
-            for j in range(PAIR):
-                w = a0[:, PAIR * c + j, :].bitcast(F32)
-                for u in range(2):
-                    nc.tensor.transpose(ps_a[:, j, u, :], w[:, u::2], ident[:])
+        def turn_a0(k):
+            w = a0[:, k, :].bitcast(F32)
+            for u in range(2):
+                nc.tensor.transpose(ps_y[:, 0, u, :], w[:, u::2], ident[:])
 
-        def copy_a0(c):
-            nc.scalar.copy(out=words(pick(a0t, c)), in_=ps_a[:].rearrange("p j u m -> p j m u"))
+        def copy_a0(k):
+            nc.scalar.copy(out=staged(k, A0_COLS).bitcast(F32).rearrange("p (m u) -> p m u", u=2),
+                           in_=ps_y[:, 0].rearrange("p u m -> p m u"))
 
-        def quant_a0(c):
-            nc.vector.quantize_mx(out=pick(a0q, c)[:].rearrange("p j m -> p (j m)").bitcast(FP8X4),
-                                  scales=pick(a0s, c)[:].rearrange("p j m -> p (j m)"),
-                                  in_=pick(a0t, c)[:].rearrange("p j m t -> p (j m t)"))
+        def quant_a0(k):
+            quant(k, A0_COLS)
+
+        def quant_a(s):
+            quant(s + 2, slice(0, 256))
 
         def spectra_mm(banks, codes, scales, h):
             nc.tensor.matmul_mx(out=banks[h][:], lhsT=codes.bitcast(FP8X4), lhsT_scale=scales,
@@ -138,50 +152,78 @@ def tile_poisson_weighted_unmixing_residual_k1_kernel(
 
         def mm1(k):
             for h in range(G):
-                spectra_mm(r0, rows(a0q, k), rows(a0s, k), h)
+                spectra_mm(res0(k), pick(codes, k)[:, A0_COLS], pick(scales, k)[:, A0_COLS], h)
 
         def sub0(k, h):
-            nc.vector.tensor_tensor(out=wide[k][:, half(h)], in0=rows(p0, k)[:, half(h)], in1=r0[h][:], op=SUB)
+            nc.vector.tensor_tensor(out=wide[k][:, half(h)], in0=rows(p0, k)[:, half(h)], in1=res0(k)[h][:], op=SUB)
+
+        def widen_p0(k):
+            nc.scalar.copy(out=wide[k][:, half(0)].rearrange("m (t p) -> m t p", t=4),
+                           in_=rows(p0, k)[:, half(0)].rearrange("m (p t) -> m t p", t=4))
+
+        def negate_r0(k):
+            nc.scalar.activation(out=pick(neg_r, k)[:], in_=r0[0][:].rearrange("m (p t) -> m t p", t=4),
+                                 func=mybir.ActivationFunctionType.Copy, scale=-1.0)
+
+        def turn_sub0(k):
+            for t in range(4):
+                cols = slice(P * t, P * (t + 1))
+                nc.tensor.matmul(turned[:, cols], lhsT=wide[k][:, cols], rhs=ident[:], start=True, stop=False, is_transpose=True)
+                nc.tensor.matmul(turned[:, cols], lhsT=pick(neg_r, k)[:, t, :], rhs=ident[:], start=False, stop=True, is_transpose=True)
+
+        def turn_v0(k):
+            w = rows(v0, k).bitcast(F32)
+            for u in range(2):
+                nc.tensor.transpose(ps_e[:, 0, u, :], w[:, u:256:2], ident[:])
+
+        def copy_v0(k):
+            nc.scalar.copy(out=pick(v0t, k)[:].rearrange("p m t -> p (m t)").bitcast(F32).rearrange("p (m u) -> p m u", u=2),
+                           in_=ps_e[:, 0].rearrange("p u m -> p m u"))
+
+        def weigh0_turned(k):
+            nc.vector.tensor_tensor(out=staged(k + 3, E_COLS)[:, half(0)].rearrange("p (m t) -> p m t", t=4),
+                                    in0=turned.rearrange("p (t m) -> p m t", t=4), in1=pick(v0t, k)[:], op=MULT)
 
         def weigh0(engine, k, cols):
             engine.tensor_tensor(out=pick(e_bf, k)[:, cols], in0=wide[k][:, cols], in1=rows(v0, k)[:, cols], op=MULT)
 
         def turn_e(k):
             w = pick(e_bf, k)[:].bitcast(F32)
-            for g in range(G):
+            for g in range(1 if k in TURNED else 0, G):
                 for u in range(2):
                     nc.tensor.transpose(ps_e[:, g, u, :], w[:, 256 * g + u : 256 * (g + 1) : 2], ident[:])
 
         def copy_e(k):
-            nc.scalar.copy(out=words(pick(e_t, k)), in_=ps_e[:].rearrange("p g u m -> p g m u"))
+            gs = slice(1 if k in TURNED else 0, G)
+            nc.scalar.copy(out=staged(k + 3, E_COLS).bitcast(F32).rearrange("p (g m u) -> p g m u", g=G, u=2)[:, gs],
+                           in_=ps_e[:, gs].rearrange("p g u m -> p g m u"))
 
         def quant_e(k):
-            nc.vector.quantize_mx(out=pick(e_q, k)[:].rearrange("p g m -> p (g m)").bitcast(FP8X4),
-                                  scales=pick(e_s, k)[:].rearrange("p g m -> p (g m)"),
-                                  in_=pick(e_t, k)[:].rearrange("p g m t -> p (g m t)"))
+            quant(k + 3, E_COLS)
 
         def mm2(k):
             for t in range(4):
                 for g in range(G):
+                    cols = slice(E_COLS.start + P * g, E_COLS.start + P * (g + 1))
                     nc.tensor.matmul_mx(out=grad[:, t, :], lhsT=uw[:, g, t, :].bitcast(FP4X4), lhsT_scale=us[:, g, t, :],
-                                        rhs=pick(e_q, k)[:, g, :].bitcast(FP8X4), rhs_scale=pick(e_s, k)[:, g, :],
+                                        rhs=pick(codes, k + 3)[:, cols].bitcast(FP8X4), rhs_scale=pick(scales, k + 3)[:, cols],
                                         start=(g == 0), stop=(g == G - 1))
 
         def update(k):
             for t in range(4):
                 nc.vector.scalar_tensor_tensor(out=pick(a1, k)[:, t, :], in0=grad[:, t, :], scalar=step_sb[:, t : t + 1],
-                                               in1=pick(a0t, k // PAIR)[:, k % PAIR, :, t], op0=MULT, op1=ADD)
+                                               in1=staged(k, A0_COLS)[:, t::4], op0=MULT, op1=ADD)
 
         def interleave_a1(k):
-            nc.scalar.copy(out=pick(a1t, k)[:].rearrange("p (m i) t -> p m t i", i=4),
+            nc.scalar.copy(out=staged(k + 5, A1_COLS).rearrange("p (m i t) -> p m t i", i=4, t=4),
                            in_=pick(a1, k)[:].rearrange("p t (m i) -> p m t i", i=4))
 
         def quant_a1(k):
-            nc.vector.quantize_mx(out=pick(a1q, k)[:].bitcast(FP8X4), scales=pick(a1s, k)[:], in_=pick(a1t, k)[:].rearrange("p m t -> p (m t)"))
+            quant(k + 5, A1_COLS)
 
         def mm3(k):
             for h in range(G):
-                spectra_mm(res1(k), pick(a1q, k)[:], pick(a1s, k)[:], h)
+                spectra_mm(res1(k), pick(codes, k + 5)[:, A1_COLS], pick(scales, k + 5)[:, A1_COLS], h)
 
         def sub1(k, h):
             nc.vector.tensor_tensor(out=pick(d1, k)[:, half(h)], in0=rows(p1, k)[:, half(h)], in1=res1(k)[h][:], op=SUB)
@@ -216,13 +258,14 @@ def tile_poisson_weighted_unmixing_residual_k1_kernel(
 
         def copy_y(k, gs=range(G)):
             sel = slice(gs[0], gs[-1] + 1)
-            nc.scalar.copy(out=words(pick(y_t, k))[:, sel], in_=y_bank(k, gs[0])[:, sel].rearrange("p g u m -> p g m u"))
+            dst = pick(y_t, k // PAIR)[:, sel, k % PAIR].rearrange("p g m t -> p g (m t)").bitcast(F32)
+            nc.scalar.copy(out=dst.rearrange("p g (m u) -> p g m u", u=2), in_=y_bank(k, gs[0])[:, sel].rearrange("p g u m -> p g m u"))
 
-        def quant_y(k, gs=range(G)):
-            cols = slice(P * k, P * (k + 1))
+        def quant_y(k, n, gs=range(G)):
+            cols = slice(P * k, P * (k + n))
             for g in gs:
                 nc.vector.quantize_mx(out=y_q[:, g, cols].bitcast(FP8X4), scales=y_s[:, g, cols],
-                                      in_=pick(y_t, k)[:, g, :, :].rearrange("p m t -> p (m t)"))
+                                      in_=pick(y_t, k // PAIR)[:, g, k % PAIR : k % PAIR + n].rearrange("p j m t -> p (j m t)"))
 
         def store_planes(k):
             if k + 1 in WORD_STORES:
@@ -235,7 +278,7 @@ def tile_poisson_weighted_unmixing_residual_k1_kernel(
                 cols = slice(P * (SCALE_STORES[i - 1] if i else 0), P * (k + 1))
                 for q in range(4):
                     dst = out_2[:, 4 * q : 4 * q + 4, cols].rearrange("g r m -> r g m")
-                    nc.sync.dma_start(out=dst.bitcast(I32), in_=y_s[32 * q : 32 * q + 4, :, cols].bitcast(I32))
+                    (nc.scalar if k == NT - 1 and q % 2 else nc.sync).dma_start(out=dst.bitcast(I32), in_=y_s[32 * q : 32 * q + 4, :, cols].bitcast(I32))
 
         def sort_u_words():
             nc.vector.tensor_copy(out=uw[:].rearrange("p g t (m b) -> p g t m b", b=2),
@@ -253,18 +296,31 @@ def tile_poisson_weighted_unmixing_residual_k1_kernel(
                                   in_=u_scales[:, 4 * q : 4 * q + 4, :].rearrange("g r n -> r g n").bitcast(I32))
 
         def load_s(h):
-            nc.sync.dma_start(out=s_raw[h][:], in_=S.rearrange("(p j) c -> p j c", j=4)[:, :, half(h)])
+            nc.sync.dma_start(out=s_raw[h], in_=S.rearrange("(p j) c -> p j c", j=4)[:, :, half(h)])
 
         def load_step():
             nc.sync.dma_start(out=step_sb[:], in_=step.rearrange("(p t) -> p t", t=4))
 
         def mm1h(k, h):
-            spectra_mm(r0, rows(a0q, k), rows(a0s, k), h)
+            spectra_mm(res0(k), pick(codes, k)[:, A0_COLS], pick(scales, k)[:, A0_COLS], h)
 
         def each(k, *stages):
             if 0 <= k < NT:
                 for stage in stages:
                     stage(k)
+
+        def first_half(s):
+            if s in TURNED:
+                weigh0_turned(s)
+            else:
+                sub0(s, 0)
+
+        def lo(s):
+            return 512 if s in TURNED else 0
+
+        def turned_only(k, *stages):
+            if k in TURNED:
+                each(k, *stages)
 
         ctx.enter_context(tc.manual_schedule())
 
@@ -273,215 +329,246 @@ def tile_poisson_weighted_unmixing_residual_k1_kernel(
         load_u_words()
         load_a0(0, 2)
         load_s(0)
-        load_s(1)
         sort_u_words()
+        load_s(1)
         load_rows(p0, P0, 0, 1)
-        interleave_s(nc.vector.tensor_copy, 1)
-        interleave_s(nc.vector.tensor_copy, 0)
+        turn_a0(0)
         load_a0(2, 4)
         load_rows(v0, V0, 0, 1)
-        load_u_scales()
         load_rows(p0, P0, 1, 1)
+        copy_a0(0)
+        quant_a0(0)
+        load_u_scales()
         load_rows(v0, V0, 1, 1)
         load_step()
+        turn_a0(1)
+        interleave_s(nc.vector.tensor_copy, 1)
+        interleave_s(nc.scalar.copy, 3)
+        copy_a0(1)
+        interleave_s(nc.vector.tensor_copy, 0)
+        interleave_s(nc.vector.tensor_copy, 2)
         load_a0(4, 8)
+        quant_s(0)
         load_rows(p0, P0, 2, 2)
         load_rows(v0, V0, 2, 2)
         load_rows(p0, P0, 4, 2)
-        load_rows(v0, V0, 4, 2)
-        load_rows(p1, P1, 0, 2)
-        turn_a0(0)
-        load_rows(v1, V1, 0, 2)
-        load_rows(p0, P0, 6, 2)
-        interleave_s(nc.vector.tensor_copy, 2)
-        quant_s(0)
-        load_rows(v0, V0, 6, 2)
-        copy_a0(0)
-        load_a0(8, 12)
-        quant_a0(0)
-        interleave_s(nc.scalar.copy, 3)
-        load_rows(p1, P1, 2, 2)
-        mm1h(0, 0)
         quant_s(1)
-        mm1h(0, 1)
-        sort_u_scales()
-        load_rows(v1, V1, 2, 2)
-        sub0(0, 0)
-        sub0(0, 1)
-        weigh0(nc.vector, 0, slice(0, 1024))
-        turn_a0(1)
-        mm1(1)
-        copy_a0(1)
-        turn_e(0)
-        copy_e(0)
-        sub0(1, 1)
-        sub0(1, 0)
-        quant_a0(1)
-        weigh0(nc.vector, 1, slice(0, 1024))
-        load_rows(p0, P0, 8, 2)
-        quant_e(0)
         turn_a0(2)
+        load_rows(v0, V0, 4, 2)
+        quant_a0(1)
+        sort_u_scales()
+        load_rows(p1, P1, 0, 2)
+        load_rows(v1, V1, 0, 2)
         copy_a0(2)
-        load_rows(v0, V0, 8, 2)
+        mm1h(0, 1)
+        load_rows(p0, P0, 6, 2)
+        sub0(0, 1)
+        mm1h(0, 0)
+        load_rows(v0, V0, 6, 2)
+        sub0(0, 0)
+        quant_a0(2)
+        load_a0(8, 12)
+        turn_a0(3)
+        mm1(1)
+        weigh0(nc.vector, 0, slice(0, 1024))
+        sub0(1, 0)
+        turn_e(0)
+        sub0(1, 1)
+        load_rows(p1, P1, 2, 2)
+        load_rows(v1, V1, 2, 2)
+        copy_a0(3)
+        copy_e(0)
+        quant_a0(3)
+        turn_a0(4)
+        quant_e(0)
+        weigh0(nc.vector, 1, slice(0, 1024))
+        copy_a0(4)
         mm1(2)
-        sub0(2, 0)
-        sub0(2, 1)
         mm2(0)
+        sub0(2, 0)
+        turn_a0(5)
+        sub0(2, 1)
         turn_e(1)
         update(0)
-        weigh0(nc.vector, 2, slice(320, 1024))
-        load_rows(p1, P1, 4, 2)
+        load_rows(p0, P0, 8, 2)
+        load_rows(v0, V0, 8, 2)
         copy_e(1)
-        quant_e(1)
-        turn_a0(3)
-        load_rows(v1, V1, 4, 2)
-        interleave_a1(0)
-        quant_a0(2)
-        copy_a0(3)
+        quant_a0(4)
+        load_rows(p1, P1, 4, 2)
+        copy_a0(5)
         mm1(3)
-        mm2(1)
+        quant_e(1)
+        weigh0(nc.vector, 2, slice(320, 1024))
+        turn_v0(4)
+        interleave_a1(0)
         sub0(3, 0)
+        quant_a(3)
+        load_rows(v1, V1, 4, 2)
+        mm2(1)
         weigh0(nc.gpsimd, 2, slice(0, 320))
-        quant_a1(0)
-        turn_e(2)
         sub0(3, 1)
-        update(1)
-        weigh0(nc.vector, 3, slice(320, 1024))
+        copy_v0(4)
+        turn_e(2)
+        mm1(4)
+        widen_p0(4)
         copy_e(2)
+        turn_a0(6)
+        update(1)
+        widen_p0(5)
+        turn_v0(5)
         quant_e(2)
         weigh0(nc.gpsimd, 3, slice(0, 320))
+        negate_r0(4)
+        weigh0(nc.vector, 3, slice(320, 1024))
+        sub0(4, 1)
+        copy_a0(6)
+        copy_v0(5)
         mm3(0)
-        mm1(4)
-        quant_a0(3)
-        interleave_a1(1)
-        quant_a1(1)
-        sub0(4, 0)
-        load_rows(p0, P0, 10, 2)
         sub1(0, 1)
-        mm2(2)
+        interleave_a1(1)
         sub1(0, 0)
+        load_rows(p0, P0, 10, 2)
+        mm2(2)
+        widen_p0(6)
         load_rows(v0, V0, 10, 2)
+        update(2)
+        turn_e(3)
+        turn_sub0(4)
         load_rows(p1, P1, 6, 2)
         load_rows(v1, V1, 6, 2)
-        turn_e(3)
-        sub0(4, 1)
-        weigh0(nc.gpsimd, 4, slice(0, 512))
-        mm3(1)
+        turn_a0(7)
         mm1(5)
         copy_e(3)
-        update(2)
+        widen_p0(7)
+        turn_v0(6)
+        copy_a0(7)
+        copy_v0(6)
+        weigh0(nc.gpsimd, 4, slice(512, 768))
+        quant_a(4)
+        negate_r0(5)
+        weigh0_turned(4)
+        mm3(1)
         interleave_a1(2)
         quant_e(3)
+        weigh0(nc.vector, 4, slice(768, 1024))
         mm2(3)
-        weigh0(nc.vector, 4, slice(512, 1024))
         for s in range(5, NT - 1):
+            weigh1(nc.gpsimd, s - 5, slice(0, C))
+            if s + 2 >= NT:
+                quant_a1(s - 3)
+            if s in (6, 8):
+                load_rows(v1, V1, s + 2, PAIR)
+            each(s + 3, turn_a0)
+            turned_only(s, turn_sub0)
+            sub0(s, 1)
+            each(s + 3, copy_a0)
+            turn_e(s - 1)
+            turned_only(s + 2, turn_v0)
+            sub1(s - 4, 0)
+            sub1(s - 4, 1)
+            turned_only(s + AHEAD, widen_p0)
+            update(s - 2)
+            first_half(s)
             if s in (6, 8):
                 load_rows(p1, P1, s + 2, PAIR)
-                load_rows(v1, V1, s + 2, PAIR)
-            weigh1(nc.gpsimd, s - 5, slice(0, C))
-            if s in (5, 7):
-                turn_a0((s + 3) // 2)
-                copy_a0((s + 3) // 2)
-            each(s - 6, turn_y, copy_y)
-            each(s - 1, turn_e, copy_e)
-            for h in HALVES:
-                sub0(s, h)
+            if s in QY:
+                quant_y(s - QY[0], PAIR)
+            store_y(s - 5)
+            if s + 2 < NT:
+                quant_a(s)
+            copy_e(s - 1)
             mm1(s + 1)
-            for h in HALVES:
-                sub1(s - 4, h)
-            update(s - 2)
-            each(s - 5, store_y, round_y)
+            each(s - 6, turn_y)
+            mm3(s - 3)
             interleave_a1(s - 2)
-            each(s - 3, quant_a1, mm3)
-            each(s - 1, quant_e, mm2)
-            if s in (6, 8):
-                quant_a0(s // 2 + 1)
-            if s >= 6:
-                quant_y(s - 6, [0])
-            weigh0(nc.vector, s, slice(0, C))
-            if s >= 6:
-                quant_y(s - 6, [1])
-                store_planes(s - 6)
-        sub1(7, 0)
+            quant_e(s - 1)
+            turned_only(s + 2, copy_v0)
+            mm2(s - 1)
+            each(s - 6, copy_y)
+            turned_only(s + 1, negate_r0)
+            round_y(s - 5)
+            weigh0(nc.vector, s, slice(lo(s), C))
         sub0(11, 1)
-        turn_y(5)
         turn_e(10)
-        sub1(7, 1)
-        update(9)
-        sub0(11, 0)
-        quant_a1(8)
-        copy_y(5)
+        sub1(7, 0)
+        turn_sub0(11)
+        turn_y(5)
         copy_e(10)
+        update(9)
+        sub1(7, 1)
         interleave_a1(9)
-        quant_y(5)
+        weigh0_turned(11)
+        quant_a1(8)
         quant_e(10)
-        weigh0(nc.vector, 11, slice(0, 1024))
         weigh1(nc.gpsimd, 6, slice(0, 1024))
+        store_planes(3)
         mm3(8)
-        round_y(6)
         quant_a1(9)
+        copy_y(5)
+        quant_y(4, 2)
+        weigh0(nc.vector, 11, slice(512, 1024))
         mm2(10)
+        round_y(6)
         turn_e(11)
-        mm3(9)
-        weigh1(nc.gpsimd, 7, slice(0, 1024))
-        sub1(8, 0)
-        turn_y(6)
         copy_e(11)
+        sub1(8, 0)
+        mm3(9)
         sub1(8, 1)
         update(10)
         sub1(9, 0)
-        interleave_a1(10)
-        copy_y(6)
         sub1(9, 1)
-        round_y(7)
-        store_y(7)
-        quant_e(11)
+        store_y(6)
+        interleave_a1(10)
+        weigh1(nc.gpsimd, 7, slice(0, 1024))
         quant_a1(10)
-        mm2(11)
-        turn_y(7)
+        turn_y(6)
+        copy_y(6)
+        round_y(7)
+        quant_e(11)
         weigh1(nc.vector, 8, slice(0, 1024))
-        weigh1(nc.gpsimd, 9, slice(0, 576))
-        round_y(8)
-        quant_y(6)
-        store_y(8)
         mm3(10)
+        mm2(11)
+        sub1(10, 0)
         update(11)
-        weigh1(nc.vector, 9, slice(576, 1024))
+        turn_y(7)
+        store_y(7)
+        copy_y(7)
+        store_y(8)
+        sub1(10, 1)
+        quant_y(6, 2)
         interleave_a1(11)
         quant_a1(11)
-        copy_y(7)
-        round_y(9)
-        sub1(10, 1)
-        quant_y(7)
-        mm3(11)
-        turn_y(9)
-        store_y(9)
-        sub1(10, 0)
-        sub1(11, 0)
-        turn_y(8)
+        weigh1(nc.gpsimd, 9, slice(0, 576))
+        weigh1(nc.vector, 9, slice(576, 1024))
         weigh1(nc.vector, 10, slice(0, 704))
-        sub1(11, 1)
-        weigh1_rounded(11, 0)
-        weigh1(nc.vector, 11, slice(0, 1024))
+        mm3(11)
         store_planes(7)
-        copy_y(9)
+        round_y(8)
+        round_y(9)
         weigh1(nc.gpsimd, 10, slice(704, 1024))
-        weigh1_rounded(11, 1)
-        store_y(6)
+        turn_y(8)
+        store_y(9)
+        sub1(11, 0)
+        sub1(11, 1)
         round_y(10)
-        turn_y(10)
-        copy_y(8)
-        quant_y(8)
+        weigh1_rounded(11, 0)
         store_y(10)
+        copy_y(8)
+        turn_y(9)
+        weigh1(nc.vector, 11, slice(0, 1024))
+        copy_y(9)
+        turn_y(10)
         copy_y(10)
-        quant_y(9)
-        store_y(11)
-        quant_y(10)
+        weigh1_rounded(11, 1)
         turn_y(11, [0])
+        quant_y(8, 2)
+        store_y(11)
+        quant_y(10, 1)
         copy_y(11, [0])
         turn_y(11, [1])
-        copy_y(11, [1])
+        store_planes(9)
         store_planes(10)
-        quant_y(11, [1])
-        quant_y(11, [0])
+        quant_y(11, 1, [0])
+        copy_y(11, [1])
+        quant_y(11, 1, [1])
         store_planes(11)

from contextlib import ExitStack

import concourse.mybir as mybir
from concourse.masks import make_identity

M, F, C = 1536, 512, 1024
FLOPS = 3 * 2 * M * F * C

F32 = mybir.dt.float32
BF16 = mybir.dt.bfloat16
I32 = mybir.dt.int32
U32 = mybir.dt.uint32
U8 = mybir.dt.uint8
FP8X4 = mybir.dt.float8_e4m3fn_x4
FP4X4 = mybir.dt.float4_e2m1fn_x4
MULT = mybir.AluOpType.mult
ADD = mybir.AluOpType.add
SUB = mybir.AluOpType.subtract

P = 128
NT = M // P
G = C // 512
PAIR = 2
IN0_RING = 4
FIRST_V = 8
ALT0 = ()
TURNED = range(4, 12)
AHEAD = 3
QY = (8, 10)
FILL0 = 0
FILL1 = 0
FILL2 = 320
FILL3 = 320
FILL4 = 256
GSPLIT = 576
GSPLIT2 = 704
WORD_STORES = (4, 8, 10, 11, 12)
SCALE_STORES = (8, 12)


def tile_poisson_weighted_unmixing_residual_k1_kernel(
    tc, A0, S, u_words, u_scales, step, P0, V0, P1, V1, out_0, out_1, out_2
):
    nc = tc.nc
    with ExitStack() as ctx:
        sb = ctx.enter_context(tc.tile_pool(name="sb", bufs=1))
        ps = ctx.enter_context(tc.psum_pool(name="ps", bufs=1))

        def ring(name, n, shape, dtype):
            return [sb.tile(shape, dtype, name="%s%d" % (name, i), align_bytes=64) for i in range(n)]

        def one(name, shape, dtype):
            return ring(name, 1, shape, dtype)[0]

        ident = one("ident", [P, P], F32)
        step_sb = one("step", [P, 4], BF16)
        uw_raw = one("uw_raw", [P, G, 2 * F], U8)
        us_raw = one("us_raw", [P, G, F], U8)
        uw = one("uw", [P, G, 4, 2 * P], U8)
        us = one("us", [P, G, 4, P], U8)
        stage = ring("stage", 6, [P, 2048], BF16)
        s_raw = [stage[2 + h][:].rearrange("p (j c) -> p j c", j=4) for h in range(G)]
        s_grp = [stage[4 + h][:].rearrange("p (c j) -> p c j", j=4) for h in range(G)]
        codes = ring("codes", 3, [P, 512], U32)
        scales = ring("scales", 3, [P, 512], U8)
        s_q = ring("s_q", G, [P, 512], U32)
        s_sc = ring("s_sc", G, [P, 512], U8)
        a0 = one("a0", [P, NT, F], BF16)
        p0 = ring("p0_", IN0_RING, [P, PAIR, C], BF16)
        v0 = ring("v0_", IN0_RING, [P, PAIR, C], BF16)
        p1 = ring("p1_", NT // PAIR - 2, [P, PAIR, C], BF16)
        v1 = ring("v1_", NT // PAIR, [P, PAIR, C], BF16)
        wide = ring("wide", NT, [P, C], F32)
        d1 = ring("d1_", 4, [P, C], F32)
        neg_r = ring("neg_r", 2, [P, 4, P], F32)
        v0t = ring("v0t", 3, [P, P, 4], BF16)
        e_bf = ring("e_bf", 2, [P, C], BF16)
        a1 = ring("a1_", 2, [P, 4, P], BF16)
        y_bf = ring("y_bf", 3, [P, C], BF16)
        y_t = ring("y_t", 2, [P, G, PAIR, P, 4], BF16)
        y_q = one("y_q", [P, G, M], U32)
        y_s = one("y_s", [P, G, M], U8)

        r0 = [ps.tile([P, 512], F32, name="r0_%d" % h) for h in range(G)]
        r1 = [ps.tile([P, 512], F32, name="r1_%d" % h) for h in range(G)]
        grad = ps.tile([P, 4, P], F32, name="grad")
        ps_a = ps.tile([P, G, 2, P], F32, name="ps_a")
        ps_e = ps.tile([P, G, 2, P], F32, name="ps_e")
        ps_y = ps.tile([P, G, 2, P], F32, name="ps_y")

        turned = ps_a[:].rearrange("p g u m -> p (g u m)")

        def pick(tiles, k):
            return tiles[k % len(tiles)]

        def rows(tiles, k):
            return pick(tiles, k // PAIR)[:, k % PAIR, :]

        def half(h):
            return slice(0, C) if h is None else slice(512 * h, 512 * (h + 1))

        def y_of(k):
            return pick(d1, k - 1) if k in (9, 10) else pick(wide, k + 4)

        def res0(k):
            return r1 if k in ALT0 else r0

        def res1(k):
            return r0 if k in (9, 11) else r1

        A1_COLS, A0_COLS, E_COLS = slice(0, 128), slice(128, 256), slice(256, 512)

        def staged(slot, cols):
            return pick(stage, slot)[:, 4 * cols.start : 4 * cols.stop]

        def quant(slot, cols):
            nc.vector.quantize_mx(out=pick(codes, slot)[:, cols].bitcast(FP8X4), scales=pick(scales, slot)[:, cols], in_=staged(slot, cols))

        def load_rows(tiles, src, k0, n):
            dst = pick(tiles, k0 // PAIR)[:, k0 % PAIR : k0 % PAIR + n, :]
            nc.sync.dma_start(out=dst, in_=src[P * k0 : P * (k0 + n), :].rearrange("(k p) c -> p k c", p=P))

        def load_a0(k0, k1):
            nc.sync.dma_start(out=a0[:, k0:k1, :], in_=A0[P * k0 : P * k1, :].rearrange("(k p) f -> p k f", p=P))

        def interleave_s(engine_copy, q):
            h, cols = q // 2, slice(256 * (q % 2), 256 * (q % 2 + 1))
            engine_copy(out=s_grp[h][:, cols, :].rearrange("p (c i) j -> p c j i", i=4),
                        in_=s_raw[h][:, :, cols].rearrange("p j (c i) -> p c j i", i=4))

        def quant_s(h):
            nc.vector.quantize_mx(out=s_q[h][:].bitcast(FP8X4), scales=s_sc[h][:], in_=stage[4 + h][:])

        def turn_a0(k):
            w = a0[:, k, :].bitcast(F32)
            for u in range(2):
                nc.tensor.transpose(ps_y[:, 0, u, :], w[:, u::2], ident[:])

        def copy_a0(k):
            nc.scalar.copy(out=staged(k, A0_COLS).bitcast(F32).rearrange("p (m u) -> p m u", u=2),
                           in_=ps_y[:, 0].rearrange("p u m -> p m u"))

        def quant_a0(k):
            quant(k, A0_COLS)

        def quant_a(s):
            quant(s + 2, slice(0, 256))

        def spectra_mm(banks, codes, scales, h):
            nc.tensor.matmul_mx(out=banks[h][:], lhsT=codes.bitcast(FP8X4), lhsT_scale=scales,
                                rhs=s_q[h][:].bitcast(FP8X4), rhs_scale=s_sc[h][:], start=True, stop=True)

        def mm1(k):
            for h in range(G):
                spectra_mm(res0(k), pick(codes, k)[:, A0_COLS], pick(scales, k)[:, A0_COLS], h)

        def sub0(k, h):
            nc.vector.tensor_tensor(out=wide[k][:, half(h)], in0=rows(p0, k)[:, half(h)], in1=res0(k)[h][:], op=SUB)

        def widen_p0(k):
            nc.scalar.copy(out=wide[k][:, half(0)].rearrange("m (t p) -> m t p", t=4),
                           in_=rows(p0, k)[:, half(0)].rearrange("m (p t) -> m t p", t=4))

        def negate_r0(k):
            nc.scalar.activation(out=pick(neg_r, k)[:], in_=r0[0][:].rearrange("m (p t) -> m t p", t=4),
                                 func=mybir.ActivationFunctionType.Copy, scale=-1.0)

        def turn_sub0(k):
            for t in range(4):
                cols = slice(P * t, P * (t + 1))
                nc.tensor.matmul(turned[:, cols], lhsT=wide[k][:, cols], rhs=ident[:], start=True, stop=False, is_transpose=True)
                nc.tensor.matmul(turned[:, cols], lhsT=pick(neg_r, k)[:, t, :], rhs=ident[:], start=False, stop=True, is_transpose=True)

        def turn_v0(k):
            w = rows(v0, k).bitcast(F32)
            for u in range(2):
                nc.tensor.transpose(ps_e[:, 0, u, :], w[:, u:256:2], ident[:])

        def copy_v0(k):
            nc.scalar.copy(out=pick(v0t, k)[:].rearrange("p m t -> p (m t)").bitcast(F32).rearrange("p (m u) -> p m u", u=2),
                           in_=ps_e[:, 0].rearrange("p u m -> p m u"))

        def weigh0_turned(k):
            nc.vector.tensor_tensor(out=staged(k + 3, E_COLS)[:, half(0)].rearrange("p (m t) -> p m t", t=4),
                                    in0=turned.rearrange("p (t m) -> p m t", t=4), in1=pick(v0t, k)[:], op=MULT)

        def weigh0(engine, k, cols):
            engine.tensor_tensor(out=pick(e_bf, k)[:, cols], in0=wide[k][:, cols], in1=rows(v0, k)[:, cols], op=MULT)

        def turn_e(k):
            w = pick(e_bf, k)[:].bitcast(F32)
            for g in range(1 if k in TURNED else 0, G):
                for u in range(2):
                    nc.tensor.transpose(ps_e[:, g, u, :], w[:, 256 * g + u : 256 * (g + 1) : 2], ident[:])

        def copy_e(k):
            gs = slice(1 if k in TURNED else 0, G)
            nc.scalar.copy(out=staged(k + 3, E_COLS).bitcast(F32).rearrange("p (g m u) -> p g m u", g=G, u=2)[:, gs],
                           in_=ps_e[:, gs].rearrange("p g u m -> p g m u"))

        def quant_e(k):
            quant(k + 3, E_COLS)

        def mm2(k):
            for t in range(4):
                for g in range(G):
                    cols = slice(E_COLS.start + P * g, E_COLS.start + P * (g + 1))
                    nc.tensor.matmul_mx(out=grad[:, t, :], lhsT=uw[:, g, t, :].bitcast(FP4X4), lhsT_scale=us[:, g, t, :],
                                        rhs=pick(codes, k + 3)[:, cols].bitcast(FP8X4), rhs_scale=pick(scales, k + 3)[:, cols],
                                        start=(g == 0), stop=(g == G - 1))

        def update(k):
            for t in range(4):
                nc.vector.scalar_tensor_tensor(out=pick(a1, k)[:, t, :], in0=grad[:, t, :], scalar=step_sb[:, t : t + 1],
                                               in1=staged(k, A0_COLS)[:, t::4], op0=MULT, op1=ADD)

        def interleave_a1(k):
            nc.scalar.copy(out=staged(k + 5, A1_COLS).rearrange("p (m i t) -> p m t i", i=4, t=4),
                           in_=pick(a1, k)[:].rearrange("p t (m i) -> p m t i", i=4))

        def quant_a1(k):
            quant(k + 5, A1_COLS)

        def mm3(k):
            for h in range(G):
                spectra_mm(res1(k), pick(codes, k + 5)[:, A1_COLS], pick(scales, k + 5)[:, A1_COLS], h)

        def sub1(k, h):
            nc.vector.tensor_tensor(out=pick(d1, k)[:, half(h)], in0=rows(p1, k)[:, half(h)], in1=res1(k)[h][:], op=SUB)

        def weigh1(engine, k, cols):
            engine.tensor_tensor(out=y_of(k)[:, cols], in0=pick(d1, k)[:, cols], in1=rows(v1, k)[:, cols], op=MULT)

        def pair_order(ap):
            return ap.rearrange("m (q u e) -> m u q e", u=2, e=2)

        def weigh1_rounded(k, g):
            dst = pick(y_bf, k)[:].rearrange("m (u q e) -> m u q e", u=2, e=2)[:, :, P * g : P * (g + 1), :]
            nc.vector.tensor_tensor(out=dst, in0=pair_order(pick(d1, k)[:, half(g)]), in1=pair_order(rows(v1, k)[:, half(g)]), op=MULT)

        def store_y(k):
            nc.sync.dma_start(out=out_0[P * k : P * (k + 1), :], in_=y_of(k)[:])

        def round_y(k):
            nc.scalar.copy(out=pick(y_bf, k)[:].rearrange("m (u q e) -> m u q e", u=2, e=2),
                           in_=pair_order(y_of(k)[:]))

        def y_bank(k, g):
            if k < 8:
                return ps_y
            return (ps_y, ps_a, ps_e)[(k + (g if k == NT - 1 else 0)) % 3]

        def turn_y(k, gs=range(G)):
            w = pick(y_bf, k)[:].bitcast(F32)
            for g in gs:
                for u in range(2):
                    nc.tensor.transpose(y_bank(k, g)[:, g, u, :], w[:, 256 * u + P * g : 256 * u + P * (g + 1)], ident[:])

        def copy_y(k, gs=range(G)):
            sel = slice(gs[0], gs[-1] + 1)
            dst = pick(y_t, k // PAIR)[:, sel, k % PAIR].rearrange("p g m t -> p g (m t)").bitcast(F32)
            nc.scalar.copy(out=dst.rearrange("p g (m u) -> p g m u", u=2), in_=y_bank(k, gs[0])[:, sel].rearrange("p g u m -> p g m u"))

        def quant_y(k, n, gs=range(G)):
            cols = slice(P * k, P * (k + n))
            for g in gs:
                nc.vector.quantize_mx(out=y_q[:, g, cols].bitcast(FP8X4), scales=y_s[:, g, cols],
                                      in_=pick(y_t, k // PAIR)[:, g, k % PAIR : k % PAIR + n].rearrange("p j m t -> p (j m t)"))

        def store_planes(k):
            if k + 1 in WORD_STORES:
                i = WORD_STORES.index(k + 1)
                cols = slice(P * (WORD_STORES[i - 1] if i else 0), P * (k + 1))
                dst = out_1.rearrange("g p m t -> p g (m t)").bitcast(I32)
                nc.sync.dma_start(out=dst[:, :, cols], in_=y_q[:, :, cols].bitcast(I32))
            if k + 1 in SCALE_STORES:
                i = SCALE_STORES.index(k + 1)
                cols = slice(P * (SCALE_STORES[i - 1] if i else 0), P * (k + 1))
                for q in range(4):
                    dst = out_2[:, 4 * q : 4 * q + 4, cols].rearrange("g r m -> r g m")
                    (nc.scalar if k == NT - 1 and q % 2 else nc.sync).dma_start(out=dst.bitcast(I32), in_=y_s[32 * q : 32 * q + 4, :, cols].bitcast(I32))

        def sort_u_words():
            nc.vector.tensor_copy(out=uw[:].rearrange("p g t (m b) -> p g t m b", b=2),
                                  in_=uw_raw[:].rearrange("p g (m t b) -> p g t m b", t=4, b=2))

        def sort_u_scales():
            nc.vector.tensor_copy(out=us[:], in_=us_raw[:].rearrange("p g (m t) -> p g t m", t=4))

        def load_u_words():
            nc.sync.dma_start(out=uw_raw[:].bitcast(I32), in_=u_words.rearrange("g p n -> p g n").bitcast(I32))

        def load_u_scales():
            for q in range(4):
                nc.sync.dma_start(out=us_raw[32 * q : 32 * q + 4, :, :].bitcast(I32),
                                  in_=u_scales[:, 4 * q : 4 * q + 4, :].rearrange("g r n -> r g n").bitcast(I32))

        def load_s(h):
            nc.sync.dma_start(out=s_raw[h], in_=S.rearrange("(p j) c -> p j c", j=4)[:, :, half(h)])

        def load_step():
            nc.sync.dma_start(out=step_sb[:], in_=step.rearrange("(p t) -> p t", t=4))

        def mm1h(k, h):
            spectra_mm(res0(k), pick(codes, k)[:, A0_COLS], pick(scales, k)[:, A0_COLS], h)

        def each(k, *stages):
            if 0 <= k < NT:
                for stage in stages:
                    stage(k)

        def first_half(s):
            if s in TURNED:
                weigh0_turned(s)
            else:
                sub0(s, 0)

        def lo(s):
            return 512 if s in TURNED else 0

        def turned_only(k, *stages):
            if k in TURNED:
                each(k, *stages)

        ctx.enter_context(tc.manual_schedule())

        nc.vector.memset(us_raw[:].rearrange("p g n -> p (g n)").bitcast(I32), 0)
        make_identity(nc, ident[:])
        load_u_words()
        load_a0(0, 2)
        load_s(0)
        sort_u_words()
        load_s(1)
        load_rows(p0, P0, 0, 1)
        turn_a0(0)
        load_a0(2, 4)
        load_rows(v0, V0, 0, 1)
        load_rows(p0, P0, 1, 1)
        copy_a0(0)
        quant_a0(0)
        load_u_scales()
        load_rows(v0, V0, 1, 1)
        load_step()
        turn_a0(1)
        interleave_s(nc.vector.tensor_copy, 1)
        interleave_s(nc.scalar.copy, 3)
        copy_a0(1)
        interleave_s(nc.vector.tensor_copy, 0)
        interleave_s(nc.vector.tensor_copy, 2)
        load_a0(4, 8)
        quant_s(0)
        load_rows(p0, P0, 2, 2)
        load_rows(v0, V0, 2, 2)
        load_rows(p0, P0, 4, 2)
        quant_s(1)
        turn_a0(2)
        load_rows(v0, V0, 4, 2)
        quant_a0(1)
        sort_u_scales()
        load_rows(p1, P1, 0, 2)
        load_rows(v1, V1, 0, 2)
        copy_a0(2)
        mm1h(0, 1)
        load_rows(p0, P0, 6, 2)
        sub0(0, 1)
        mm1h(0, 0)
        load_rows(v0, V0, 6, 2)
        sub0(0, 0)
        quant_a0(2)
        load_a0(8, 12)
        turn_a0(3)
        mm1(1)
        weigh0(nc.vector, 0, slice(0, 1024))
        sub0(1, 0)
        turn_e(0)
        sub0(1, 1)
        load_rows(p1, P1, 2, 2)
        load_rows(v1, V1, 2, 2)
        copy_a0(3)
        copy_e(0)
        quant_a0(3)
        turn_a0(4)
        quant_e(0)
        weigh0(nc.vector, 1, slice(0, 1024))
        copy_a0(4)
        mm1(2)
        mm2(0)
        sub0(2, 0)
        turn_a0(5)
        sub0(2, 1)
        turn_e(1)
        update(0)
        load_rows(p0, P0, 8, 2)
        load_rows(v0, V0, 8, 2)
        copy_e(1)
        quant_a0(4)
        load_rows(p1, P1, 4, 2)
        copy_a0(5)
        mm1(3)
        quant_e(1)
        weigh0(nc.vector, 2, slice(320, 1024))
        turn_v0(4)
        interleave_a1(0)
        sub0(3, 0)
        quant_a(3)
        load_rows(v1, V1, 4, 2)
        mm2(1)
        weigh0(nc.gpsimd, 2, slice(0, 320))
        sub0(3, 1)
        copy_v0(4)
        turn_e(2)
        mm1(4)
        widen_p0(4)
        copy_e(2)
        turn_a0(6)
        update(1)
        widen_p0(5)
        turn_v0(5)
        quant_e(2)
        weigh0(nc.gpsimd, 3, slice(0, 320))
        negate_r0(4)
        weigh0(nc.vector, 3, slice(320, 1024))
        sub0(4, 1)
        copy_a0(6)
        copy_v0(5)
        mm3(0)
        sub1(0, 1)
        interleave_a1(1)
        sub1(0, 0)
        load_rows(p0, P0, 10, 2)
        mm2(2)
        widen_p0(6)
        load_rows(v0, V0, 10, 2)
        update(2)
        turn_e(3)
        turn_sub0(4)
        load_rows(p1, P1, 6, 2)
        load_rows(v1, V1, 6, 2)
        turn_a0(7)
        mm1(5)
        copy_e(3)
        widen_p0(7)
        turn_v0(6)
        copy_a0(7)
        copy_v0(6)
        weigh0(nc.gpsimd, 4, slice(512, 768))
        quant_a(4)
        negate_r0(5)
        weigh0_turned(4)
        mm3(1)
        interleave_a1(2)
        quant_e(3)
        weigh0(nc.vector, 4, slice(768, 1024))
        mm2(3)
        for s in range(5, NT - 1):
            weigh1(nc.gpsimd, s - 5, slice(0, C))
            if s + 2 >= NT:
                quant_a1(s - 3)
            if s in (6, 8):
                load_rows(v1, V1, s + 2, PAIR)
            each(s + 3, turn_a0)
            turned_only(s, turn_sub0)
            sub0(s, 1)
            each(s + 3, copy_a0)
            turn_e(s - 1)
            turned_only(s + 2, turn_v0)
            sub1(s - 4, 0)
            sub1(s - 4, 1)
            turned_only(s + AHEAD, widen_p0)
            update(s - 2)
            first_half(s)
            if s in (6, 8):
                load_rows(p1, P1, s + 2, PAIR)
            if s in QY:
                quant_y(s - QY[0], PAIR)
            store_y(s - 5)
            if s + 2 < NT:
                quant_a(s)
            copy_e(s - 1)
            mm1(s + 1)
            each(s - 6, turn_y)
            mm3(s - 3)
            interleave_a1(s - 2)
            quant_e(s - 1)
            turned_only(s + 2, copy_v0)
            mm2(s - 1)
            each(s - 6, copy_y)
            turned_only(s + 1, negate_r0)
            round_y(s - 5)
            weigh0(nc.vector, s, slice(lo(s), C))
        sub0(11, 1)
        turn_e(10)
        sub1(7, 0)
        turn_sub0(11)
        turn_y(5)
        copy_e(10)
        update(9)
        sub1(7, 1)
        interleave_a1(9)
        weigh0_turned(11)
        quant_a1(8)
        quant_e(10)
        weigh1(nc.gpsimd, 6, slice(0, 1024))
        store_planes(3)
        mm3(8)
        quant_a1(9)
        copy_y(5)
        quant_y(4, 2)
        weigh0(nc.vector, 11, slice(512, 1024))
        mm2(10)
        round_y(6)
        turn_e(11)
        copy_e(11)
        sub1(8, 0)
        mm3(9)
        sub1(8, 1)
        update(10)
        sub1(9, 0)
        sub1(9, 1)
        store_y(6)
        interleave_a1(10)
        weigh1(nc.gpsimd, 7, slice(0, 1024))
        quant_a1(10)
        turn_y(6)
        copy_y(6)
        round_y(7)
        quant_e(11)
        weigh1(nc.vector, 8, slice(0, 1024))
        mm3(10)
        mm2(11)
        sub1(10, 0)
        update(11)
        turn_y(7)
        store_y(7)
        copy_y(7)
        store_y(8)
        sub1(10, 1)
        quant_y(6, 2)
        interleave_a1(11)
        quant_a1(11)
        weigh1(nc.gpsimd, 9, slice(0, 576))
        weigh1(nc.vector, 9, slice(576, 1024))
        weigh1(nc.vector, 10, slice(0, 704))
        mm3(11)
        store_planes(7)
        round_y(8)
        round_y(9)
        weigh1(nc.gpsimd, 10, slice(704, 1024))
        turn_y(8)
        store_y(9)
        sub1(11, 0)
        sub1(11, 1)
        round_y(10)
        weigh1_rounded(11, 0)
        store_y(10)
        copy_y(8)
        turn_y(9)
        weigh1(nc.vector, 11, slice(0, 1024))
        copy_y(9)
        turn_y(10)
        copy_y(10)
        weigh1_rounded(11, 1)
        turn_y(11, [0])
        quant_y(8, 2)
        store_y(11)
        quant_y(10, 1)
        copy_y(11, [0])
        turn_y(11, [1])
        store_planes(9)
        store_planes(10)
        quant_y(11, 1, [0])
        copy_y(11, [1])
        quant_y(11, 1, [1])
        store_planes(11)
